import numpy as np
import ml_dtypes


def mxq(x, axis, fmt="e4m3"):
    dtype, down = {"e4m3": (ml_dtypes.float8_e4m3fn, 7), "e5m2": (ml_dtypes.float8_e5m2, 14)}[fmt]
    v = np.moveaxis(np.asarray(x, np.float32).astype(ml_dtypes.bfloat16).astype(np.float64), axis, -1)
    blocks = v.reshape(v.shape[:-1] + (-1, 32))
    amax = np.abs(blocks).max(-1, keepdims=True)
    byte = np.maximum(np.where(amax > 0, np.frexp(amax)[1] - 1 + 127, 0) - down, 1)
    scale = np.exp2(byte - 127.0)
    codes = (blocks / scale).astype(np.float32).astype(dtype).astype(np.float64)
    return np.moveaxis((codes * scale).reshape(v.shape), -1, axis)


WIDE = False


def mx_kscale(k):
    if not WIDE:
        return np.ones(k)
    levels = np.array([10, -10, 5, -5, 0])
    if k % 512:
        return np.exp2(np.random.permutation(np.resize(levels, k // 32))).repeat(32)
    a = np.empty((k // 512, 16))
    for p in range(k // 512):
        a[p, :8] = np.random.permutation(np.resize(levels, 8))
        for g in range(8):
            far = levels[np.abs(levels - a[p, g]) >= 10]
            a[p, g + 8] = far[np.random.randint(len(far))]
    return np.exp2(a.ravel()).repeat(32)


def f64(x):
    return np.asarray(x).astype(np.float64)


def striped(idx):
    return np.tile(idx.reshape(-1, 16).T, (8, 1)).astype(np.uint16)


def unstriped(offs):
    return offs[:16].T.reshape(-1).astype(np.int64)


def striped8(idx):
    return np.concatenate([x.reshape(-1, 16).T for x in idx]).astype(np.uint16)


def runs(offs, k):
    lists = np.stack([offs[16 * r : 16 * r + 16].T.reshape(-1) for r in range(8)]).astype(np.int64)
    return lists[np.arange(k) % 512 // 64]


def pack_weight(w):
    k, n = w.shape
    w = f64(np.asarray(w, np.float32).astype(ml_dtypes.bfloat16)).reshape(k // 32, 32, n)
    amax = np.abs(w).max(1)
    byte = np.clip(np.where(amax > 0, np.frexp(amax)[1] - 1 + 127 - 7, 1), 1, 254)
    scaled = (w * np.exp2(127.0 - byte)[:, None, :]).reshape(k, n).astype(np.float32)
    words = np.ascontiguousarray(scaled.reshape(k // 512, 128, 4, n).transpose(0, 1, 3, 2)).astype(ml_dtypes.float8_e4m3fn).view(np.uint8)
    return words, np.ascontiguousarray(byte.astype(np.uint8).reshape(k // 512, 16, n))


def unpack_weight(words, scales):
    g, p, n, _ = words.shape
    vals = np.ascontiguousarray(words).view(ml_dtypes.float8_e4m3fn).astype(np.float64) * np.repeat(np.exp2(scales.astype(np.float64) - 127.0), 8, axis=1)[..., None]
    return vals.transpose(0, 1, 3, 2).reshape(g * 512, n)


E2M1 = np.array([0.0, 0.5, 1.0, 1.5, 2.0, 3.0, 4.0, 6.0, -0.0, -0.5, -1.0, -1.5, -2.0, -3.0, -4.0, -6.0])


def pack_fp4(w):
    k, n = w.shape
    w = f64(np.asarray(w, np.float32).astype(ml_dtypes.bfloat16)).reshape(k // 32, 32, n)
    amax = np.abs(w).max(1)
    mant, ex = np.frexp(amax / 6.0)
    byte = np.clip(np.where(amax > 0, np.where(mant > 0.5, ex, ex - 1) + 127, 1), 1, 254)
    scaled = (w * np.exp2(127.0 - byte)[:, None, :]).reshape(k, n).astype(np.float32)
    c = np.ascontiguousarray(scaled.reshape(k // 512, 128, 4, n).transpose(0, 1, 3, 2)).astype(ml_dtypes.float4_e2m1fn).view(np.uint8) & 0xF
    words = (c[..., 0::2] | (c[..., 1::2] << 4)).reshape(k // 512, 128, 2 * n)
    return np.ascontiguousarray(words), np.ascontiguousarray(byte.astype(np.uint8).reshape(k // 512, 16, n))


def unpack_fp4(words, scales):
    g, _, n = scales.shape
    words = np.ascontiguousarray(words).reshape(g, 128, n, 2)
    nib = np.empty((g, 128, n, 4), np.uint8)
    nib[..., 0::2] = words & 0xF
    nib[..., 1::2] = words >> 4
    vals = E2M1[nib] * np.repeat(np.exp2(scales.astype(np.float64) - 127.0), 8, axis=1)[..., None]
    return vals.transpose(0, 1, 3, 2).reshape(g * 512, n)


def sigmoid(v):
    return 1.0 / (1.0 + np.exp(-np.maximum(v, -700.0)))

def planes(y):
    n, m = y.shape
    v = y.astype(np.float32).astype(ml_dtypes.bfloat16).astype(np.float64).reshape(n // 32, 32, m)
    top = np.abs(v).max(1)
    byte = np.clip(np.where(top > 0, np.frexp(top)[1] - 1 + 127 - 7, 1), 1, 254)
    codes = (v * np.exp2(127.0 - byte)[:, None, :]).reshape(n, m).astype(np.float32).astype(ml_dtypes.float8_e4m3fn).view(np.uint8)
    words = codes.reshape(n // 512, 128, 4, m).transpose(0, 1, 3, 2)
    return np.ascontiguousarray(words), np.ascontiguousarray(byte.astype(np.uint8).reshape(n // 512, 16, m))


K, T, S, H, G = 512, 2048, 512, 512, 2048


def setup_inputs():
    n = np.random.standard_normal
    s = mx_kscale(K)[:, None]
    packed_xT = pack_weight(n((K, T)) * s)
    packed_w1 = pack_fp4(n((K, H)) / np.sqrt(K) / s)
    packed_dT = pack_weight(n((K, G)) / s)
    return {
        "x_words": packed_xT[0],
        "x_scales": packed_xT[1],
        "w1_words": packed_w1[0],
        "w1_scales": packed_w1[1],
        "gs": (np.random.uniform(0.5, 1.5, (K, 1)) * s).astype(np.float32),
        "d_words": packed_dT[0],
        "d_scales": packed_dT[1],
        "offs": striped(np.random.permutation(T)[:S]),
        "n1": striped8(np.stack([np.random.permutation(S) for _ in range(8)])),
        "n2": striped8(np.stack([np.random.permutation(S) for _ in range(8)])),
        "k1": striped8(np.random.randint(0, G, (8, H))),
        "n3": striped8(np.stack([np.random.permutation(S) for _ in range(8)])),
    }


def reference(x_words, x_scales, w1_words, w1_scales, gs, d_words, d_scales, offs, n1, n2, k1, n3):
    d_k1 = unpack_weight(d_words, d_scales)[np.arange(K)[:, None], runs(k1, K)]
    xq = unpack_weight(x_words, x_scales)[:, unstriped(offs)]
    y = unpack_fp4(w1_words, w1_scales).T @ xq
    st = y[np.arange(H)[:, None], runs(n1, H)] - y
    z = f64(gs) * (y * (sigmoid(st[np.arange(H)[:, None], runs(n2, H)])))
    h = 0.0625 * ((d_k1.T @ mxq(z, 0, "e4m3")))
    pa = h[np.arange(H)[:, None], runs(n3, H)]
    out_0 = (2.0 * (h * pa)) / ((h) ** 2 + (pa) ** 2 + 0.5)
    return (out_0,) + planes(out_0)

@@ -1,0 +1,279 @@
+from contextlib import ExitStack
+
+import concourse.mybir as mybir
+from concourse.masks import make_identity
+
+K, T, S, H, G = 512, 2048, 512, 512, 2048
+FLOPS = 2 * K * H * S + 2 * H * H * S
+
+F32 = mybir.dt.float32
+BF16 = mybir.dt.bfloat16
+I32 = mybir.dt.int32
+U32 = mybir.dt.uint32
+U16 = mybir.dt.uint16
+U8 = mybir.dt.uint8
+FP8X4 = mybir.dt.float8_e4m3fn_x4
+FP4X4 = mybir.dt.float4_e2m1fn_x4
+ACT = mybir.ActivationFunctionType
+ALU = mybir.AluOpType
+
+P = 128
+PACK = 4
+HALF = S // 2
+LIST_COLS = HALF // 16
+
+
+def tile_picked_densehopdharm_none_po_kernel(
+    tc, x_words, x_scales, w1_words, w1_scales, gs, d_words, d_scales, offs, n1, n2, k1, n3, out_0, out_1, out_2
+):
+    nc = tc.nc
+    with ExitStack() as ctx:
+        lists = ctx.enter_context(tc.tile_pool(name="lists", bufs=1))
+        sb = ctx.enter_context(tc.tile_pool(name="sb", bufs=1))
+        ps = ctx.enter_context(tc.psum_pool(name="ps", bufs=1))
+
+        def tile(name, shape, dtype, tag=None, bufs=1):
+            return sb.tile(shape, dtype, name=name, tag=tag or name, bufs=bufs, align_bytes=64)
+
+        def half_list(lst, c):
+            return lst[:, c * LIST_COLS : (c + 1) * LIST_COLS]
+
+        def cols(c):
+            return slice(c * HALF, (c + 1) * HALF)
+
+        xs_tab = tile("xs_tab", [P, T], U8)
+        ws_raw = tile("ws_raw", [P, H], U8)
+        ds_tab = tile("ds_tab", [P, G], U8)
+        warm = tile("warm", [P, 1], F32)
+        warm_out = tile("warm_out", [P, 1], F32)
+        nc.vector.memset(warm[:], 0.0)
+        nc.vector.memset(ds_tab[:].bitcast(I32), 0)
+
+        offs_t = lists.tile([P, S // 16], U16, name="offs_t")
+        n1_t = lists.tile([P, S // 16], U16, name="n1_t")
+        n2_t = lists.tile([P, S // 16], U16, name="n2_t")
+        k1_t = lists.tile([P, H // 16], U16, name="k1_t")
+        n3_t = lists.tile([P, S // 16], U16, name="n3_t")
+
+        xw_tab = tile("xw_tab", [P, T], U32)
+        dw_tab = tile("dw_tab", [P, G], U32)
+        ww_raw = tile("ww_raw", [P, 2 * H], U8)
+        gs_t = tile("gs_t", [P, PACK], F32)
+
+        def load_scale_rows(eng, dst, scales, q):
+            eng.dma_start(
+                dst[:].bitcast(I32)[32 * q : 32 * q + 32, :],
+                scales[0].bitcast(I32)[4 * q : 4 * q + 4, :].partition_broadcast(8),
+            )
+
+        nc.sync.dma_start(offs_t[:], offs)
+        for q in range(2):
+            load_scale_rows(nc.sync, xs_tab, x_scales, q)
+        nc.sync.dma_start(xw_tab[:].bitcast(I32), x_words[0].rearrange("p n t -> p (n t)").bitcast(I32))
+        nc.scalar.dma_start(ww_raw[:].bitcast(I32), w1_words[0].bitcast(I32))
+        for q in range(2, 4):
+            load_scale_rows(nc.scalar, xs_tab, x_scales, q)
+        for q in range(4):
+            load_scale_rows(nc.scalar, ws_raw, w1_scales, q)
+        nc.scalar.activation(warm_out[:], warm[:], ACT.Sigmoid)
+        nc.sync.dma_start(k1_t[:], k1)
+        for e in range(2):
+            nc.sync.dma_start(ds_tab[:].bitcast(I32)[e:P:16, :], d_scales[0].bitcast(I32)[e:16:2, :])
+        nc.sync.dma_start(n1_t[:], n1)
+        nc.sync.dma_start(n2_t[:], n2)
+        nc.sync.dma_start(dw_tab[:].bitcast(I32), d_words[0].rearrange("p n t -> p (n t)").bitcast(I32))
+        nc.sync.dma_start(gs_t[:], gs.rearrange("(p t) o -> p (t o)", t=PACK))
+        nc.sync.dma_start(n3_t[:], n3)
+
+        ident = tile("ident", [P, P], F32)
+        make_identity(nc, ident[:])
+        ww = tile("ww", [P, 2 * H], U8)
+        ws = tile("ws", [P, H], U8)
+        nc.gpsimd.tensor_copy(
+            ww[:].rearrange("p (t m b) -> p t m b", t=PACK, b=2),
+            ww_raw[:].rearrange("p (m t b) -> p t m b", t=PACK, b=2),
+        )
+        xs = tile("xs", [P, S], U8)
+        xw = tile("xw", [P, S], U32)
+        nc.vector.tensor_copy(xs[:], xs_tab[:].indirect(offs_t[:]))
+        nc.gpsimd.tensor_copy(
+            ws[:].rearrange("p (t m) -> p t m", t=PACK), ws_raw[:].rearrange("p (m t) -> p t m", t=PACK)
+        )
+        nc.vector.tensor_copy(xw[:], xw_tab[:].indirect(offs_t[:]))
+
+        y_ps = [ps.tile([P, S], F32, name=f"y_ps{t}") for t in range(PACK)]
+        y_again = [tile(f"y_again{t}", [P, S], F32) for t in range(PACK)]
+        y = [tile(f"y{t}", [P, S], F32) for t in range(PACK)]
+        for t in range(PACK):
+            nc.tensor.matmul_mx(
+                out=y_ps[t][:],
+                lhsT=ww[:, 2 * P * t : 2 * P * (t + 1)].bitcast(FP4X4),
+                lhsT_scale=ws[:, P * t : P * (t + 1)],
+                rhs=xw[:].bitcast(FP8X4),
+                rhs_scale=xs[:],
+                start=True,
+                stop=True,
+            )
+            nc.scalar.copy(y[t][:], y_ps[t][:])
+            nc.scalar.copy(y_again[t][:], y_ps[t][:])
+
+        ds_pick = tile("ds_pick", [P, H], U8)
+        ds = tile("ds", [P, H], U8)
+        nc.vector.tensor_copy(ds_pick[:], ds_tab[:].indirect(k1_t[:]))
+        nc.vector.tensor_copy(
+            ds[:].rearrange("p (t m) -> p t m", t=PACK), ds_pick[:].rearrange("p (m t) -> p t m", t=PACK)
+        )
+        for e in range(2):
+            nc.sync.dma_start(ds[:].bitcast(I32)[2 + e : P : 32, :], ds[:].bitcast(I32)[16 + e : P : 32, :])
+
+        st = [tile(f"st{t}", [P, S], F32) for t in range(PACK)]
+        gate = [tile(f"gate{t}", [P, S], F32) for t in range(PACK)]
+        for t in range(PACK):
+            for c in range(2):
+                nc.vector.tensor_tensor(
+                    st[t][:, cols(c)], y[t][:].indirect(half_list(n1_t, c)), y_again[t][:, cols(c)], ALU.subtract
+                )
+            nc.scalar.activation(gate[t][:, cols(0)], st[t][:].indirect(half_list(n2_t, 0)), ACT.Sigmoid)
+        for t in range(PACK):
+            nc.scalar.activation(gate[t][:, cols(1)], st[t][:].indirect(half_list(n2_t, 1)), ACT.Sigmoid)
+        nc.scalar.activation(warm_out[:], gate[PACK - 1][:, S - 1 : S], ACT.Abs_reciprocal_sqrt)
+
+        dw_pick = tile("dw_pick", [P, H], U32)
+        dw = tile("dw", [P, H], U32)
+        nc.vector.tensor_copy(dw_pick[:], dw_tab[:].indirect(k1_t[:]))
+        nc.vector.tensor_copy(
+            dw[:].bitcast(I32).rearrange("p (t m) -> p t m", t=PACK),
+            dw_pick[:].bitcast(I32).rearrange("p (m t) -> p t m", t=PACK),
+        )
+
+        h = [tile(f"h{t}", [P, S], F32) for t in range(PACK)]
+        h_ps = [[ps.tile([P, 2, HALF], F32, name=f"h_ps{c}{u}") for u in range(2)] for c in range(2)]
+        for c in range(2):
+            z = tile(f"z{c}", [P, PACK, HALF], F32)
+            for t in range(PACK):
+                nc.vector.scalar_tensor_tensor(
+                    z[:, t, :], y_ps[t][:, cols(c)], gs_t[:, t : t + 1], gate[t][:, cols(c)], ALU.mult, ALU.mult
+                )
+            zb = tile(f"zb{c}", [P, HALF, PACK], BF16)
+            (nc.vector.tensor_copy if c == 0 else nc.vector.tensor_copy)(
+                zb[:].rearrange("p (a i) t -> p a t i", i=4), z[:].rearrange("p t (a i) -> p a t i", i=4)
+            )
+            zw = tile(f"zw{c}", [P, HALF], U32)
+            zs = tile(f"zs{c}", [P, HALF], U8)
+            nc.vector.quantize_mx(
+                out=zw[:].bitcast(FP8X4), scales=zs[:], in_=zb[:].rearrange("p j t -> p (j t)")
+            )
+            for t in range(PACK):
+                nc.tensor.matmul_mx(
+                    out=h_ps[c][t // 2][:, t % 2, :],
+                    lhsT=dw[:, P * t : P * (t + 1)].bitcast(FP8X4),
+                    lhsT_scale=ds[:, P * t : P * (t + 1)],
+                    rhs=zw[:].bitcast(FP8X4),
+                    rhs_scale=zs[:],
+                    start=True,
+                    stop=True,
+                )
+            for t in range(PACK):
+                if c == 1 and t < 1:
+                    nc.vector.tensor_scalar(h[t][:, cols(c)], h_ps[c][t // 2][:, t % 2, :], 0.0625, None, ALU.mult)
+                else:
+                    nc.scalar.activation(h[t][:, cols(c)], h_ps[c][t // 2][:, t % 2, :], ACT.Copy, scale=0.0625)
+
+        out_rows = out_0.rearrange("(p t) j -> p t j", t=PACK)
+        out_words = out_1[0].rearrange("p n t -> p (n t)").bitcast(I32)
+        os_ = tile("os_", [P, S], U8)
+        units = [(c, u) for c in range(2) for u in range(2)]
+        res = [tile(f"res{c}", [P, PACK, HALF], F32) for c in range(2)]
+        held = {}
+
+        def fetch(i):
+            c, u = units[i]
+            pa = tile(f"pa{i}", [P, 2, HALF], F32, tag="pa", bufs=3)
+            hh = tile(f"hh{i}", [P, 2, HALF], F32, tag="hh", bufs=4)
+            pp = tile(f"pp{i}", [P, 2, HALF], F32)
+            num = tile(f"num{i}", [P, 2, HALF], F32)
+            for v in range(2):
+                nc.vector.tensor_copy(pa[:, v, :], h[2 * u + v][:].indirect(half_list(n3_t, c)))
+            nc.scalar.activation(hh[:], h_ps[c][u][:], ACT.Square, scale=0.0625)
+            nc.scalar.activation(pp[:], pa[:], ACT.Square)
+            nc.vector.scalar_tensor_tensor(num[:], h_ps[c][u][:], 0.125, pa[:], ALU.mult, ALU.mult)
+            held[i] = (hh, pp, num)
+
+        def invert(i):
+            hh, pp, num = held[i]
+            if i < 2:
+                den_t = ps.tile([P, PACK, P], F32, name=f"den_t{i}", tag=f"y_ps{2 * i % PACK}")
+                inv_ps = ps.tile([P, PACK, P], F32, name=f"inv_ps{i}", tag=f"y_ps{(2 * i + 1) % PACK}")
+                rs_t = tile(f"rs{i}", [P, PACK, P], F32)
+                inv_t = tile(f"inv{i}", [P, PACK, P], F32)
+                for b in range(PACK):
+                    for first, term in ((True, hh), (False, pp)):
+                        nc.tensor.matmul(
+                            den_t[:, b, :],
+                            term[:].rearrange("p v j -> p (v j)")[:, b * P : (b + 1) * P],
+                            ident[:],
+                            start=first,
+                            stop=not first,
+                            is_transpose=True,
+                        )
+                nc.scalar.activation(rs_t[:], den_t[:], ACT.Abs_reciprocal_sqrt, bias=0.5)
+                nc.scalar.activation(inv_t[:], rs_t[:], ACT.Square)
+                for b in range(PACK):
+                    nc.tensor.transpose(inv_ps[:, b, :], inv_t[:, b, :], ident[:])
+                held[i] = (num, inv_ps[:].rearrange("p (v a) j -> p v (a j)", v=2))
+                return
+            den = tile(f"den{i}", [P, 2, HALF], F32)
+            rs = tile(f"rs{i}", [P, 2, HALF], F32)
+            inv = tile(f"inv{i}", [P, 2, HALF], F32)
+            nc.vector.tensor_tensor(den[:], hh[:], pp[:], ALU.add)
+            nc.scalar.activation(rs[:], den[:], ACT.Abs_reciprocal_sqrt, bias=0.5)
+            nc.scalar.activation(inv[:], rs[:], ACT.Square)
+            held[i] = (num, inv[:])
+
+        def finish(i):
+            c, u = units[i]
+            num, inv = held[i]
+            pair = slice(2 * u, 2 * u + 2)
+            if i == len(units) - 1:
+                ob = tile(f"ob{c}", [P, HALF, PACK], BF16)
+                ow = tile(f"ow{c}", [P, HALF], U32)
+                parts = [slice(0, HALF // 2), slice(HALF // 2, HALF)]
+                for part in parts:
+                    nc.vector.tensor_tensor(res[c][:, pair, part], num[:, :, part], inv[:, :, part], ALU.mult)
+                nc.sync.dma_start(out_rows[:, pair, cols(c)], res[c][:, pair, :])
+                for part in parts:
+                    (nc.vector.tensor_copy)(
+                        ob[:, part, :].rearrange("p (a i) t -> p a t i", i=4),
+                        res[c][:, :, part].rearrange("p t (a i) -> p a t i", i=4),
+                    )
+                for part in parts:
+                    nc.vector.quantize_mx(
+                        out=ow[:, part].bitcast(FP8X4),
+                        scales=os_[:, HALF + part.start : HALF + part.stop],
+                        in_=ob[:, part, :].rearrange("p j t -> p (j t)"),
+                    )
+                nc.sync.dma_start(out_words[:, cols(c)], ow[:].bitcast(I32))
+                return
+            nc.vector.tensor_tensor(res[c][:, pair, :], num[:], inv, ALU.mult)
+            nc.sync.dma_start(out_rows[:, pair, cols(c)], res[c][:, pair, :])
+            if u == 1:
+                ob = tile(f"ob{c}", [P, HALF, PACK], BF16)
+                (nc.vector.tensor_copy if c == 0 else nc.vector.tensor_copy)(
+                    ob[:].rearrange("p (a i) t -> p a t i", i=4), res[c][:].rearrange("p t (a i) -> p a t i", i=4)
+                )
+                ow = tile(f"ow{c}", [P, HALF], U32)
+                nc.vector.quantize_mx(
+                    out=ow[:].bitcast(FP8X4), scales=os_[:, cols(c)], in_=ob[:].rearrange("p j t -> p (j t)")
+                )
+                nc.sync.dma_start(out_words[:, cols(c)], ow[:].bitcast(I32))
+
+        for step in range(len(units) + 2):
+            if step < len(units):
+                fetch(step)
+            if 0 <= step - 1 < len(units):
+                invert(step - 1)
+            if 0 <= step - 2 < len(units):
+                finish(step - 2)
+        for r in range(4):
+            eng = nc.sync if r % 2 == 0 else nc.scalar
+            eng.dma_start(out_2[0].bitcast(I32)[r:16:4, :], os_[:].bitcast(I32)[r:P:32, :])

@@ -74,14 +74,14 @@ def tile_picked_densehopdharm_none_po_kernel(
         for q in range(2, 4):
             load_scale_rows(nc.scalar, xs_tab, x_scales, q)
         for q in range(4):
-            load_scale_rows(nc.scalar, ws_raw, w1_scales, q)
+            load_scale_rows(nc.scalar if q < 3 else nc.sync, ws_raw, w1_scales, q)
+        for e in range(2):
+            nc.scalar.dma_start(ds_tab[:].bitcast(I32)[e:P:16, :], d_scales[0].bitcast(I32)[e:16:2, :])
         nc.scalar.activation(warm_out[:], warm[:], ACT.Sigmoid)
         nc.sync.dma_start(k1_t[:], k1)
-        for e in range(2):
-            nc.sync.dma_start(ds_tab[:].bitcast(I32)[e:P:16, :], d_scales[0].bitcast(I32)[e:16:2, :])
+        nc.sync.dma_start(dw_tab[:].bitcast(I32), d_words[0].rearrange("p n t -> p (n t)").bitcast(I32))
         nc.sync.dma_start(n1_t[:], n1)
         nc.sync.dma_start(n2_t[:], n2)
-        nc.sync.dma_start(dw_tab[:].bitcast(I32), d_words[0].rearrange("p n t -> p (n t)").bitcast(I32))
         nc.sync.dma_start(gs_t[:], gs.rearrange("(p t) o -> p (t o)", t=PACK))
         nc.sync.dma_start(n3_t[:], n3)
 
@@ -89,20 +89,20 @@ def tile_picked_densehopdharm_none_po_kernel(
         make_identity(nc, ident[:])
         ww = tile("ww", [P, 2 * H], U8)
         ws = tile("ws", [P, H], U8)
-        nc.gpsimd.tensor_copy(
+        nc.vector.tensor_copy(
             ww[:].rearrange("p (t m b) -> p t m b", t=PACK, b=2),
             ww_raw[:].rearrange("p (m t b) -> p t m b", t=PACK, b=2),
         )
         xs = tile("xs", [P, S], U8)
         xw = tile("xw", [P, S], U32)
         nc.vector.tensor_copy(xs[:], xs_tab[:].indirect(offs_t[:]))
-        nc.gpsimd.tensor_copy(
+        nc.vector.tensor_copy(
             ws[:].rearrange("p (t m) -> p t m", t=PACK), ws_raw[:].rearrange("p (m t) -> p t m", t=PACK)
         )
         nc.vector.tensor_copy(xw[:], xw_tab[:].indirect(offs_t[:]))
 
         y_ps = [ps.tile([P, S], F32, name=f"y_ps{t}") for t in range(PACK)]
-        y_again = [tile(f"y_again{t}", [P, S], F32) for t in range(PACK)]
+        y_again = {t: tile(f"y_again{t}", [P, S], F32) for t in (0, 1, 2, 3,)}
         y = [tile(f"y{t}", [P, S], F32) for t in range(PACK)]
         for t in range(PACK):
             nc.tensor.matmul_mx(
@@ -115,7 +115,8 @@ def tile_picked_densehopdharm_none_po_kernel(
                 stop=True,
             )
             nc.scalar.copy(y[t][:], y_ps[t][:])
-            nc.scalar.copy(y_again[t][:], y_ps[t][:])
+            if t in (0, 1, 2, 3,):
+                nc.scalar.copy(y_again[t][:], y_ps[t][:])
 
         ds_pick = tile("ds_pick", [P, H], U8)
         ds = tile("ds", [P, H], U8)
@@ -126,25 +127,31 @@ def tile_picked_densehopdharm_none_po_kernel(
         for e in range(2):
             nc.sync.dma_start(ds[:].bitcast(I32)[2 + e : P : 32, :], ds[:].bitcast(I32)[16 + e : P : 32, :])
 
-        st = [tile(f"st{t}", [P, S], F32) for t in range(PACK)]
-        gate = [tile(f"gate{t}", [P, S], F32) for t in range(PACK)]
-        for t in range(PACK):
-            for c in range(2):
-                nc.vector.tensor_tensor(
-                    st[t][:, cols(c)], y[t][:].indirect(half_list(n1_t, c)), y_again[t][:, cols(c)], ALU.subtract
-                )
-            nc.scalar.activation(gate[t][:, cols(0)], st[t][:].indirect(half_list(n2_t, 0)), ACT.Sigmoid)
-        for t in range(PACK):
-            nc.scalar.activation(gate[t][:, cols(1)], st[t][:].indirect(half_list(n2_t, 1)), ACT.Sigmoid)
-        nc.scalar.activation(warm_out[:], gate[PACK - 1][:, S - 1 : S], ACT.Abs_reciprocal_sqrt)
-
         dw_pick = tile("dw_pick", [P, H], U32)
         dw = tile("dw", [P, H], U32)
         nc.vector.tensor_copy(dw_pick[:], dw_tab[:].indirect(k1_t[:]))
         nc.vector.tensor_copy(
-            dw[:].bitcast(I32).rearrange("p (t m) -> p t m", t=PACK),
-            dw_pick[:].bitcast(I32).rearrange("p (m t) -> p t m", t=PACK),
+            dw[:].bitcast(I32).rearrange("p (t a i) -> p a t i", t=PACK, i=4),
+            dw_pick[:].bitcast(I32).rearrange("p (a i t) -> p a t i", t=PACK, i=4),
         )
+
+        st = [tile(f"st{t}", [P, S], F32) for t in range(PACK)]
+        gate = [tile(f"gate{t}", [P, S], F32) for t in range(PACK)]
+        for t in range(PACK):
+            if t in (0, 1, 2, 3,):
+                for c in range(2):
+                    nc.vector.tensor_tensor(
+                        st[t][:, cols(c)], y[t][:].indirect(half_list(n1_t, c)), y_again[t][:, cols(c)], ALU.subtract
+                    )
+            else:
+                hop = tile(f"hop{t}", [P, S], F32)
+                for c in range(2):
+                    nc.vector.tensor_copy(hop[:, cols(c)], y[t][:].indirect(half_list(n1_t, c)))
+                nc.vector.tensor_tensor(st[t][:], hop[:], y_ps[t][:], ALU.subtract)
+            nc.scalar.activation(gate[t][:, cols(0)], st[t][:].indirect(half_list(n2_t, 0)), ACT.Sigmoid)
+        for t in range(PACK):
+            nc.scalar.activation(gate[t][:, cols(1)], st[t][:].indirect(half_list(n2_t, 1)), ACT.Sigmoid)
+        nc.scalar.activation(warm_out[:], gate[PACK - 1][:, S - 1 : S], ACT.Abs_reciprocal_sqrt)
 
         h = [tile(f"h{t}", [P, S], F32) for t in range(PACK)]
         h_ps = [[ps.tile([P, 2, HALF], F32, name=f"h_ps{c}{u}") for u in range(2)] for c in range(2)]
@@ -174,7 +181,7 @@ def tile_picked_densehopdharm_none_po_kernel(
                     stop=True,
                 )
             for t in range(PACK):
-                if c == 1 and t < 1:
+                if c == 1 and t < 2:
                     nc.vector.tensor_scalar(h[t][:, cols(c)], h_ps[c][t // 2][:, t % 2, :], 0.0625, None, ALU.mult)
                 else:
                     nc.scalar.activation(h[t][:, cols(c)], h_ps[c][t // 2][:, t % 2, :], ACT.Copy, scale=0.0625)
@@ -188,9 +195,9 @@ def tile_picked_densehopdharm_none_po_kernel(
 
         def fetch(i):
             c, u = units[i]
-            pa = tile(f"pa{i}", [P, 2, HALF], F32, tag="pa", bufs=3)
+            pa = tile(f"pa{i}", [P, 2, HALF], F32, tag="pa", bufs=2)
             hh = tile(f"hh{i}", [P, 2, HALF], F32, tag="hh", bufs=4)
-            pp = tile(f"pp{i}", [P, 2, HALF], F32)
+            pp = tile(f"pp{i}", [P, 2, HALF], F32, tag=f"ring{i % 2}" if i >= 2 else None)
             num = tile(f"num{i}", [P, 2, HALF], F32)
             for v in range(2):
                 nc.vector.tensor_copy(pa[:, v, :], h[2 * u + v][:].indirect(half_list(n3_t, c)))
@@ -201,10 +208,10 @@ def tile_picked_densehopdharm_none_po_kernel(
 
         def invert(i):
             hh, pp, num = held[i]
-            if i < 2:
+            if i < 3:
                 den_t = ps.tile([P, PACK, P], F32, name=f"den_t{i}", tag=f"y_ps{2 * i % PACK}")
                 inv_ps = ps.tile([P, PACK, P], F32, name=f"inv_ps{i}", tag=f"y_ps{(2 * i + 1) % PACK}")
-                rs_t = tile(f"rs{i}", [P, PACK, P], F32)
+                rs_t = tile(f"rs{i}", [P, PACK, P], F32, tag=f"ring{i}" if i < 2 else None)
                 inv_t = tile(f"inv{i}", [P, PACK, P], F32)
                 for b in range(PACK):
                     for first, term in ((True, hh), (False, pp)):

@@ -203,12 +203,16 @@ def tile_picked_densehopdharm_none_po_kernel(
                 nc.vector.tensor_copy(pa[:, v, :], h[2 * u + v][:].indirect(half_list(n3_t, c)))
             nc.scalar.activation(hh[:], h_ps[c][u][:], ACT.Square, scale=0.0625)
             nc.scalar.activation(pp[:], pa[:], ACT.Square)
-            nc.vector.scalar_tensor_tensor(num[:], h_ps[c][u][:], 0.125, pa[:], ALU.mult, ALU.mult)
+            if i < 2:
+                for v in range(2):
+                    nc.gpsimd.tensor_tensor(num[:, v, :], h[2 * u + v][:, cols(c)], pa[:, v, :], ALU.mult)
+            else:
+                nc.vector.scalar_tensor_tensor(num[:], h_ps[c][u][:], 0.0625, pa[:], ALU.mult, ALU.mult)
             held[i] = (hh, pp, num)
 
         def invert(i):
             hh, pp, num = held[i]
-            if i < 3:
+            if i < 2:
                 den_t = ps.tile([P, PACK, P], F32, name=f"den_t{i}", tag=f"y_ps{2 * i % PACK}")
                 inv_ps = ps.tile([P, PACK, P], F32, name=f"inv_ps{i}", tag=f"y_ps{(2 * i + 1) % PACK}")
                 rs_t = tile(f"rs{i}", [P, PACK, P], F32, tag=f"ring{i}" if i < 2 else None)
@@ -223,7 +227,7 @@ def tile_picked_densehopdharm_none_po_kernel(
                             stop=not first,
                             is_transpose=True,
                         )
-                nc.scalar.activation(rs_t[:], den_t[:], ACT.Abs_reciprocal_sqrt, bias=0.5)
+                nc.scalar.activation(rs_t[:], den_t[:], ACT.Abs_reciprocal_sqrt, bias=0.25, scale=0.5)
                 nc.scalar.activation(inv_t[:], rs_t[:], ACT.Square)
                 for b in range(PACK):
                     nc.tensor.transpose(inv_ps[:, b, :], inv_t[:, b, :], ident[:])
@@ -233,8 +237,9 @@ def tile_picked_densehopdharm_none_po_kernel(
             rs = tile(f"rs{i}", [P, 2, HALF], F32)
             inv = tile(f"inv{i}", [P, 2, HALF], F32)
             nc.vector.tensor_tensor(den[:], hh[:], pp[:], ALU.add)
-            nc.scalar.activation(rs[:], den[:], ACT.Abs_reciprocal_sqrt, bias=0.5)
-            nc.scalar.activation(inv[:], rs[:], ACT.Square)
+            for part in ([slice(0, HALF // 2), slice(HALF // 2, HALF)] if i == len(units) - 1 else [slice(0, HALF)]):
+                nc.scalar.activation(rs[:, :, part], den[:, :, part], ACT.Abs_reciprocal_sqrt, bias=0.25, scale=0.5)
+                nc.scalar.activation(inv[:, :, part], rs[:, :, part], ACT.Square)
             held[i] = (num, inv[:])
 
         def finish(i):

from contextlib import ExitStack

import concourse.mybir as mybir
from concourse.masks import make_identity

K, T, S, H, G = 512, 2048, 512, 512, 2048
FLOPS = 2 * K * H * S + 2 * H * H * S

F32 = mybir.dt.float32
BF16 = mybir.dt.bfloat16
I32 = mybir.dt.int32
U32 = mybir.dt.uint32
U16 = mybir.dt.uint16
U8 = mybir.dt.uint8
FP8X4 = mybir.dt.float8_e4m3fn_x4
FP4X4 = mybir.dt.float4_e2m1fn_x4
ACT = mybir.ActivationFunctionType
ALU = mybir.AluOpType

P = 128
PACK = 4
HALF = S // 2
LIST_COLS = HALF // 16


def tile_picked_densehopdharm_none_po_kernel(
    tc, x_words, x_scales, w1_words, w1_scales, gs, d_words, d_scales, offs, n1, n2, k1, n3, out_0, out_1, out_2
):
    nc = tc.nc
    with ExitStack() as ctx:
        lists = ctx.enter_context(tc.tile_pool(name="lists", bufs=1))
        sb = ctx.enter_context(tc.tile_pool(name="sb", bufs=1))
        ps = ctx.enter_context(tc.psum_pool(name="ps", bufs=1))

        def tile(name, shape, dtype, tag=None, bufs=1):
            return sb.tile(shape, dtype, name=name, tag=tag or name, bufs=bufs, align_bytes=64)

        def half_list(lst, c):
            return lst[:, c * LIST_COLS : (c + 1) * LIST_COLS]

        def cols(c):
            return slice(c * HALF, (c + 1) * HALF)

        xs_tab = tile("xs_tab", [P, T], U8)
        ws_raw = tile("ws_raw", [P, H], U8)
        ds_tab = tile("ds_tab", [P, G], U8)
        warm = tile("warm", [P, 1], F32)
        warm_out = tile("warm_out", [P, 1], F32)
        nc.vector.memset(warm[:], 0.0)
        nc.vector.memset(ds_tab[:].bitcast(I32), 0)

        offs_t = lists.tile([P, S // 16], U16, name="offs_t")
        n1_t = lists.tile([P, S // 16], U16, name="n1_t")
        n2_t = lists.tile([P, S // 16], U16, name="n2_t")
        k1_t = lists.tile([P, H // 16], U16, name="k1_t")
        n3_t = lists.tile([P, S // 16], U16, name="n3_t")

        xw_tab = tile("xw_tab", [P, T], U32)
        dw_tab = tile("dw_tab", [P, G], U32)
        ww_raw = tile("ww_raw", [P, 2 * H], U8)
        gs_t = tile("gs_t", [P, PACK], F32)

        def load_scale_rows(eng, dst, scales, q):
            eng.dma_start(
                dst[:].bitcast(I32)[32 * q : 32 * q + 32, :],
                scales[0].bitcast(I32)[4 * q : 4 * q + 4, :].partition_broadcast(8),
            )

        nc.sync.dma_start(offs_t[:], offs)
        for q in range(2):
            load_scale_rows(nc.sync, xs_tab, x_scales, q)
        nc.sync.dma_start(xw_tab[:].bitcast(I32), x_words[0].rearrange("p n t -> p (n t)").bitcast(I32))
        nc.scalar.dma_start(ww_raw[:].bitcast(I32), w1_words[0].bitcast(I32))
        for q in range(2, 4):
            load_scale_rows(nc.scalar, xs_tab, x_scales, q)
        for q in range(4):
            load_scale_rows(nc.scalar if q < 3 else nc.sync, ws_raw, w1_scales, q)
        for e in range(2):
            nc.scalar.dma_start(ds_tab[:].bitcast(I32)[e:P:16, :], d_scales[0].bitcast(I32)[e:16:2, :])
        nc.scalar.activation(warm_out[:], warm[:], ACT.Sigmoid)
        nc.sync.dma_start(k1_t[:], k1)
        nc.sync.dma_start(dw_tab[:].bitcast(I32), d_words[0].rearrange("p n t -> p (n t)").bitcast(I32))
        nc.sync.dma_start(n1_t[:], n1)
        nc.sync.dma_start(n2_t[:], n2)
        nc.sync.dma_start(gs_t[:], gs.rearrange("(p t) o -> p (t o)", t=PACK))
        nc.sync.dma_start(n3_t[:], n3)

        ident = tile("ident", [P, P], F32)
        make_identity(nc, ident[:])
        ww = tile("ww", [P, 2 * H], U8)
        ws = tile("ws", [P, H], U8)
        nc.vector.tensor_copy(
            ww[:].rearrange("p (t m b) -> p t m b", t=PACK, b=2),
            ww_raw[:].rearrange("p (m t b) -> p t m b", t=PACK, b=2),
        )
        xs = tile("xs", [P, S], U8)
        xw = tile("xw", [P, S], U32)
        nc.vector.tensor_copy(xs[:], xs_tab[:].indirect(offs_t[:]))
        nc.vector.tensor_copy(
            ws[:].rearrange("p (t m) -> p t m", t=PACK), ws_raw[:].rearrange("p (m t) -> p t m", t=PACK)
        )
        nc.vector.tensor_copy(xw[:], xw_tab[:].indirect(offs_t[:]))

        y_ps = [ps.tile([P, S], F32, name=f"y_ps{t}") for t in range(PACK)]
        y_again = {t: tile(f"y_again{t}", [P, S], F32) for t in (0, 1, 2, 3,)}
        y = [tile(f"y{t}", [P, S], F32) for t in range(PACK)]
        for t in range(PACK):
            nc.tensor.matmul_mx(
                out=y_ps[t][:],
                lhsT=ww[:, 2 * P * t : 2 * P * (t + 1)].bitcast(FP4X4),
                lhsT_scale=ws[:, P * t : P * (t + 1)],
                rhs=xw[:].bitcast(FP8X4),
                rhs_scale=xs[:],
                start=True,
                stop=True,
            )
            nc.scalar.copy(y[t][:], y_ps[t][:])
            if t in (0, 1, 2, 3,):
                nc.scalar.copy(y_again[t][:], y_ps[t][:])

        ds_pick = tile("ds_pick", [P, H], U8)
        ds = tile("ds", [P, H], U8)
        nc.vector.tensor_copy(ds_pick[:], ds_tab[:].indirect(k1_t[:]))
        nc.vector.tensor_copy(
            ds[:].rearrange("p (t m) -> p t m", t=PACK), ds_pick[:].rearrange("p (m t) -> p t m", t=PACK)
        )
        for e in range(2):
            nc.sync.dma_start(ds[:].bitcast(I32)[2 + e : P : 32, :], ds[:].bitcast(I32)[16 + e : P : 32, :])

        dw_pick = tile("dw_pick", [P, H], U32)
        dw = tile("dw", [P, H], U32)
        nc.vector.tensor_copy(dw_pick[:], dw_tab[:].indirect(k1_t[:]))
        nc.vector.tensor_copy(
            dw[:].bitcast(I32).rearrange("p (t a i) -> p a t i", t=PACK, i=4),
            dw_pick[:].bitcast(I32).rearrange("p (a i t) -> p a t i", t=PACK, i=4),
        )

        st = [tile(f"st{t}", [P, S], F32) for t in range(PACK)]
        gate = [tile(f"gate{t}", [P, S], F32) for t in range(PACK)]
        for t in range(PACK):
            if t in (0, 1, 2, 3,):
                for c in range(2):
                    nc.vector.tensor_tensor(
                        st[t][:, cols(c)], y[t][:].indirect(half_list(n1_t, c)), y_again[t][:, cols(c)], ALU.subtract
                    )
            else:
                hop = tile(f"hop{t}", [P, S], F32)
                for c in range(2):
                    nc.vector.tensor_copy(hop[:, cols(c)], y[t][:].indirect(half_list(n1_t, c)))
                nc.vector.tensor_tensor(st[t][:], hop[:], y_ps[t][:], ALU.subtract)
            nc.scalar.activation(gate[t][:, cols(0)], st[t][:].indirect(half_list(n2_t, 0)), ACT.Sigmoid)
        for t in range(PACK):
            nc.scalar.activation(gate[t][:, cols(1)], st[t][:].indirect(half_list(n2_t, 1)), ACT.Sigmoid)
        nc.scalar.activation(warm_out[:], gate[PACK - 1][:, S - 1 : S], ACT.Abs_reciprocal_sqrt)

        h = [tile(f"h{t}", [P, S], F32) for t in range(PACK)]
        h_ps = [[ps.tile([P, 2, HALF], F32, name=f"h_ps{c}{u}") for u in range(2)] for c in range(2)]
        for c in range(2):
            z = tile(f"z{c}", [P, PACK, HALF], F32)
            for t in range(PACK):
                nc.vector.scalar_tensor_tensor(
                    z[:, t, :], y_ps[t][:, cols(c)], gs_t[:, t : t + 1], gate[t][:, cols(c)], ALU.mult, ALU.mult
                )
            zb = tile(f"zb{c}", [P, HALF, PACK], BF16)
            (nc.vector.tensor_copy if c == 0 else nc.vector.tensor_copy)(
                zb[:].rearrange("p (a i) t -> p a t i", i=4), z[:].rearrange("p t (a i) -> p a t i", i=4)
            )
            zw = tile(f"zw{c}", [P, HALF], U32)
            zs = tile(f"zs{c}", [P, HALF], U8)
            nc.vector.quantize_mx(
                out=zw[:].bitcast(FP8X4), scales=zs[:], in_=zb[:].rearrange("p j t -> p (j t)")
            )
            for t in range(PACK):
                nc.tensor.matmul_mx(
                    out=h_ps[c][t // 2][:, t % 2, :],
                    lhsT=dw[:, P * t : P * (t + 1)].bitcast(FP8X4),
                    lhsT_scale=ds[:, P * t : P * (t + 1)],
                    rhs=zw[:].bitcast(FP8X4),
                    rhs_scale=zs[:],
                    start=True,
                    stop=True,
                )
            for t in range(PACK):
                if c == 1 and t < 2:
                    nc.vector.tensor_scalar(h[t][:, cols(c)], h_ps[c][t // 2][:, t % 2, :], 0.0625, None, ALU.mult)
                else:
                    nc.scalar.activation(h[t][:, cols(c)], h_ps[c][t // 2][:, t % 2, :], ACT.Copy, scale=0.0625)

        out_rows = out_0.rearrange("(p t) j -> p t j", t=PACK)
        out_words = out_1[0].rearrange("p n t -> p (n t)").bitcast(I32)
        os_ = tile("os_", [P, S], U8)
        units = [(c, u) for c in range(2) for u in range(2)]
        res = [tile(f"res{c}", [P, PACK, HALF], F32) for c in range(2)]
        held = {}

        def fetch(i):
            c, u = units[i]
            pa = tile(f"pa{i}", [P, 2, HALF], F32, tag="pa", bufs=2)
            hh = tile(f"hh{i}", [P, 2, HALF], F32, tag="hh", bufs=4)
            pp = tile(f"pp{i}", [P, 2, HALF], F32, tag=f"ring{i % 2}" if i >= 2 else None)
            num = tile(f"num{i}", [P, 2, HALF], F32)
            for v in range(2):
                nc.vector.tensor_copy(pa[:, v, :], h[2 * u + v][:].indirect(half_list(n3_t, c)))
            nc.scalar.activation(hh[:], h_ps[c][u][:], ACT.Square, scale=0.0625)
            nc.scalar.activation(pp[:], pa[:], ACT.Square)
            if i < 2:
                for v in range(2):
                    nc.gpsimd.tensor_tensor(num[:, v, :], h[2 * u + v][:, cols(c)], pa[:, v, :], ALU.mult)
            else:
                nc.vector.scalar_tensor_tensor(num[:], h_ps[c][u][:], 0.0625, pa[:], ALU.mult, ALU.mult)
            held[i] = (hh, pp, num)

        def invert(i):
            hh, pp, num = held[i]
            if i < 2:
                den_t = ps.tile([P, PACK, P], F32, name=f"den_t{i}", tag=f"y_ps{2 * i % PACK}")
                inv_ps = ps.tile([P, PACK, P], F32, name=f"inv_ps{i}", tag=f"y_ps{(2 * i + 1) % PACK}")
                rs_t = tile(f"rs{i}", [P, PACK, P], F32, tag=f"ring{i}" if i < 2 else None)
                inv_t = tile(f"inv{i}", [P, PACK, P], F32)
                for b in range(PACK):
                    for first, term in ((True, hh), (False, pp)):
                        nc.tensor.matmul(
                            den_t[:, b, :],
                            term[:].rearrange("p v j -> p (v j)")[:, b * P : (b + 1) * P],
                            ident[:],
                            start=first,
                            stop=not first,
                            is_transpose=True,
                        )
                nc.scalar.activation(rs_t[:], den_t[:], ACT.Abs_reciprocal_sqrt, bias=0.25, scale=0.5)
                nc.scalar.activation(inv_t[:], rs_t[:], ACT.Square)
                for b in range(PACK):
                    nc.tensor.transpose(inv_ps[:, b, :], inv_t[:, b, :], ident[:])
                held[i] = (num, inv_ps[:].rearrange("p (v a) j -> p v (a j)", v=2))
                return
            den = tile(f"den{i}", [P, 2, HALF], F32)
            rs = tile(f"rs{i}", [P, 2, HALF], F32)
            inv = tile(f"inv{i}", [P, 2, HALF], F32)
            nc.vector.tensor_tensor(den[:], hh[:], pp[:], ALU.add)
            for part in ([slice(0, HALF // 2), slice(HALF // 2, HALF)] if i == len(units) - 1 else [slice(0, HALF)]):
                nc.scalar.activation(rs[:, :, part], den[:, :, part], ACT.Abs_reciprocal_sqrt, bias=0.25, scale=0.5)
                nc.scalar.activation(inv[:, :, part], rs[:, :, part], ACT.Square)
            held[i] = (num, inv[:])

        def finish(i):
            c, u = units[i]
            num, inv = held[i]
            pair = slice(2 * u, 2 * u + 2)
            if i == len(units) - 1:
                ob = tile(f"ob{c}", [P, HALF, PACK], BF16)
                ow = tile(f"ow{c}", [P, HALF], U32)
                parts = [slice(0, HALF // 2), slice(HALF // 2, HALF)]
                for part in parts:
                    nc.vector.tensor_tensor(res[c][:, pair, part], num[:, :, part], inv[:, :, part], ALU.mult)
                nc.sync.dma_start(out_rows[:, pair, cols(c)], res[c][:, pair, :])
                for part in parts:
                    (nc.vector.tensor_copy)(
                        ob[:, part, :].rearrange("p (a i) t -> p a t i", i=4),
                        res[c][:, :, part].rearrange("p t (a i) -> p a t i", i=4),
                    )
                for part in parts:
                    nc.vector.quantize_mx(
                        out=ow[:, part].bitcast(FP8X4),
                        scales=os_[:, HALF + part.start : HALF + part.stop],
                        in_=ob[:, part, :].rearrange("p j t -> p (j t)"),
                    )
                nc.sync.dma_start(out_words[:, cols(c)], ow[:].bitcast(I32))
                return
            nc.vector.tensor_tensor(res[c][:, pair, :], num[:], inv, ALU.mult)
            nc.sync.dma_start(out_rows[:, pair, cols(c)], res[c][:, pair, :])
            if u == 1:
                ob = tile(f"ob{c}", [P, HALF, PACK], BF16)
                (nc.vector.tensor_copy if c == 0 else nc.vector.tensor_copy)(
                    ob[:].rearrange("p (a i) t -> p a t i", i=4), res[c][:].rearrange("p t (a i) -> p a t i", i=4)
                )
                ow = tile(f"ow{c}", [P, HALF], U32)
                nc.vector.quantize_mx(
                    out=ow[:].bitcast(FP8X4), scales=os_[:, cols(c)], in_=ob[:].rearrange("p j t -> p (j t)")
                )
                nc.sync.dma_start(out_words[:, cols(c)], ow[:].bitcast(I32))

        for step in range(len(units) + 2):
            if step < len(units):
                fetch(step)
            if 0 <= step - 1 < len(units):
                invert(step - 1)
            if 0 <= step - 2 < len(units):
                finish(step - 2)
        for r in range(4):
            eng = nc.sync if r % 2 == 0 else nc.scalar
            eng.dma_start(out_2[0].bitcast(I32)[r:16:4, :], os_[:].bitcast(I32)[r:P:32, :])
